import numpy as np, ml_dtypes
CORES = [12,28,60,100,156,228]
N = 6
import mx_ref
NC, ROOT = 256, 3
C = np.float32(0.037)
BF = ml_dtypes.bfloat16
def cut(t, i, w=512):
    return t[:, w * i:w * i + w]
def tile(rs):
    return np.stack(rs, axis=2).reshape(128, -1).astype(BF)
def pick(b):
    s = np.zeros((128, 128, 4), np.float32)
    s[np.arange(128), np.arange(128), b] = 1.0
    return mx_ref.quantize(s.reshape(128, 512).astype(BF))
def pk(c, s, i=0):
    return (np.ascontiguousarray(c[:, 512 * i:512 * i + 512]), mx_ref.live(s[:, 128 * i:128 * i + 128]))
def inputs(rng, e, E):
    def f(*shape):
        v = (rng.standard_normal(shape, dtype=np.float32) * np.exp2(rng.integers(-2, 3, shape[:-1] + (1,)))).astype(BF)
        return mx_ref.spread((v.astype(np.float32) * np.exp2(rng.integers(-E, E + 1, shape[:-2] + (1, 1))).astype(np.float32)).astype(BF), rng, e)
    def packed(k):
        c = np.zeros((N, 128, k * 512), np.uint8); s = np.zeros((N, 128, k * 128), np.uint8)
        for r in range(N):
            for i in range(k):
                a, b = mx_ref.quantize(f(128, 512)); c[r][:, 512 * i:512 * i + 512] = a; s[r][:, 128 * i:128 * i + 128] = mx_ref.plane(b, rng)
        return c, s
    d = {}
    d["wc"], d["ws"] = packed(1)
    d["a"] = f(N, 128, 512)
    d["bb"] = f(N, 128, 4 * 512)
    d["x"] = f(N, 128, 4 * NC)
    return d
def setup_inputs(rng):
    return inputs(rng, 0, 0)
def setup_inputs_blocks(rng):
    return inputs(rng, 2, 0)
def setup_inputs_wide(rng):
    return inputs(rng, 0, 3)
def reference(wc, ws, a, bb, x):
    S = [pick(t) for t in range(4)]; A = mx_ref.quantize(a[ROOT])
    V = [mx_ref.quantize(tile([mx_ref.matmul(S[t], pk(wc[j], ws[j])) + mx_ref.matmul(mx_ref.quantize(cut(bb[j], t)), A) * C for t in range(4)])) for j in range(N)]
    y = np.zeros((N, 128, N * NC), np.float32)
    for r in range(N):
        X = mx_ref.quantize(x[r])
        for j in range(N):
            y[r][:, NC * j:NC * j + NC] = mx_ref.matmul(V[j], X)
    return {"y": y}

from concourse.bass import DstId, RemoteDMATransfer
from concourse.mybir import dt, AluOpType, ActivationFunctionType

F8, U8, BF, F32 = "float8_e4m3fn_x4", "uint8", "bfloat16", "float32"
SIM = 256
NX = 256
NR = 6
C = 0.037

SCRATCH = {
    "eye": ("sbuf", [128, 516], BF),
    "at": ("sbuf", [128, 512], BF), "bt": ("sbuf", [128, 2048], BF), "xt": ("sbuf", [128, 1024], BF),
    "sc": ("sbuf", [128, 512], F8), "ss": ("sbuf", [128, 512], U8),
    "bc": ("sbuf", [128, 512], F8), "bs": ("sbuf", [128, 512], U8),
    "xc": ("sbuf", [128, 256], F8), "xs": ("sbuf", [128, 256], U8),
    "pc": ("sbuf", [128, 128], F8), "ps": ("sbuf", [128, 128], U8),
    "ac": ("sbuf", [128, 128], F8), "as_": ("sbuf", [128, 128], U8),
    "vc": ("sbuf", [128, 128 * NR], F8), "vs": ("sbuf", [128, 128 * NR], U8),
    "rc": ("sbuf", [128, 384], F8), "rs": ("sbuf", [128, 384], U8),
    "m": ("sbuf", [128, 512], F32), "vt": ("sbuf", [128, 512], BF),
    "yo": ("sbuf", [128, NX * NR], F32),
    "acc": ("psum", [128, 4096], F32),
}
SEMAPHORES = (["in_a", "in_w", "in_b", "in_x", "one", "sel", "qa", "qs", "qb", "qx", "dd", "ad", "qv", "loc",
               "arr_a", "rel_a", "rel_v", "rel_t", "st_s", "st_a"]
              + ["ba%d" % b for b in range(4)] + ["ml%d" % b for b in range(4)]
              + ["v%d" % j for j in range(NR)] + ["my%d" % j for j in range(NR)] + ["cy%d" % j for j in range(NR)])


def count(mask):
    return bin(mask).count("1")


def routes(T, topo):
    cores = T.cores
    near, far, lanes, seen = {}, {}, {}, {}
    for r in range(NR):
        c = cores[r]
        order = [(r + k) % NR for k in range(1, NR)]
        near[r] = [d for d in order if topo.may_write(c, cores[d])]
        far[r] = sorted(d for d in order if not topo.may_write(c, cores[d]))
        own = [k for k in range(SIM) if k != c and topo.host(k) == topo.host(c) and topo.chip(k) == topo.chip(c)
               and all(topo.may_write(k, cores[d]) for d in far[r])]
        here = [k for k in own if topo.die(k) == topo.die(c)]
        there = [k for k in own if topo.die(k) != topo.die(c)]
        if len(far[r]) > 2:
            h = len(far[r]) // 2
            lanes[r] = [("c", here[0], far[r][:h]), ("c", there[0], far[r][h:]),
                        ("s", there[1], far[r][:h]), ("s", here[1], far[r][h:])]
        else:
            group = tuple(far[r])
            turn = seen.get(group, 0)
            seen[group] = turn + 1
            first, second = (here, there) if turn % 2 == 0 else (there, here)
            lanes[r] = [("c", first[0], far[r]), ("s", second[0], far[r])]
    return near, far, lanes


def rank_program(g, core, T, topo):
    cores, root = T.cores, T.root
    near, far, lanes = routes(T, topo)
    rank = T.rank_of(core)
    loc = [0]

    def codes(buf, i):
        return buf[:, 128 * i:128 * i + 128].bitcast(dt.uint8)

    def plane(buf, i):
        return buf[:, 128 * i:128 * i + 128]

    def move(kind, src, to, sem, mask):
        ids = []
        for d, _ in to:
            rid, pid = topo.addr(d, core)
            ids.append(DstId(rid=rid, pnc=pid))
        loc[0] += count(mask)
        return RemoteDMATransfer(dst_ids=ids, dma_engine_mask=mask, remote_sem=sem, srcs=[src], dsts=[s for _, s in to], alu_op=0)

    def send(*moves):
        g.remote_dma_fused(list(moves), local_sem=T.sem.loc)

    def relays_of(r, kind):
        return [k for kd, k, _ in lanes[r] if kd == kind]

    def vland(kind, j):
        return codes(T.vc, j) if kind == "c" else plane(T.vs, j)

    def rland(kind, i):
        return codes(T.rc, i) if kind == "c" else plane(T.rs, i)

    def aland(kind):
        return codes(T.ac, 0) if kind == "c" else plane(T.as_, 0)

    if rank is None:
        mine = [(r, kind, dests) for r in range(NR) for kind, k, dests in lanes[r] if k == core]
        if not mine:
            return
        r, kind, dests = mine[0]
        inside = topo.mask(core, cores[r])
        out = topo.mask(core, cores[dests[0]])
        inner = count(topo.mask(cores[r], core) & ~topo.mask(cores[r], cores[near[r][0]]))
        if r == root:
            g.wait_ge(T.sem.rel_a, count(topo.mask(cores[r], core)))
            send(move(kind, rland(kind, 0), [(cores[d], aland(kind)) for d in dests], T.sem.arr_a, out))
            g.wait_ge(T.sem.rel_v, inner)
            send(move(kind, rland(kind, 1), [(relays_of(d, kind)[0], rland(kind, 2)) for d in dests], T.sem.rel_t, out))
        else:
            if root in dests:
                g.wait_ge(T.sem.rel_t, count(out))
                send(move(kind, rland(kind, 2), [(cores[r], vland(kind, root))], T.sem["v%d" % root], inside & out))
            g.wait_ge(T.sem.rel_v, inner)
            send(move(kind, rland(kind, 1), [(cores[d], vland(kind, r)) for d in dests], T.sem["v%d" % r], out))
        g.wait_ge(T.sem.loc, loc[0])
        return

    v, t, s = g.vector, g.tensor, g.scalar
    out = topo.mask(core, cores[near[rank][0]])
    full = topo.mask(core, lanes[rank][0][1])
    rest = full & ~out
    order = [rank] + [j for j in (root, far[rank][-1] if root in far[rank] else root) if j != rank]
    order = list(dict.fromkeys(order + [j for j in (far[rank] if root in far[rank] else near[rank]) if j != rank]))
    order += [j for j in [(rank - k) % NR for k in range(1, NR)] if j not in order]

    if rank == root:
        g.sync.dma_start(T.at[:], T.a[:]).then_inc(T.sem.in_a, 16)
    g.sync.dma_start(T.pc[:].bitcast(dt.uint8), T.wc[:]).then_inc(T.sem.in_w, 16)
    g.sync.dma_start(T.ps[:], T.ws[:]).then_inc(T.sem.in_w, 16)
    g.sync.dma_start(T.bt[:], T.bb[:]).then_inc(T.sem.in_b, 16)
    (g.sync if rank == root else s).dma_start(T.xt[:], T.x[:]).then_inc(T.sem.in_x, 16)

    v.memset(T.eye[:], 1.0).then_inc(T.sem.one, 1)
    if rank == root:
        v.wait_ge(T.sem.in_a, 16)
        v.quantize_mx(T.ac[:], T.as_[:], T.at[:]).then_inc(T.sem.qa, 1)
    v.wait_ge(T.sem.sel, 1)
    for b in range(4):
        v.quantize_mx(T.sc[:, 128 * b:128 * b + 128], T.ss[:, 128 * b:128 * b + 128], T.eye[:, 3 - b:515 - b]).then_inc(T.sem.qs, 1)
    v.wait_ge(T.sem.in_b, 16)
    for b in range(4):
        v.quantize_mx(T.bc[:, 128 * b:128 * b + 128], T.bs[:, 128 * b:128 * b + 128], T.bt[:, 512 * b:512 * b + 512]).then_inc(T.sem.qb, 1)

    def pack_x():
        v.wait_ge(T.sem.in_x, 16)
        v.quantize_mx(T.xc[:], T.xs[:], T.xt[:]).then_inc(T.sem.qx, 1)

    if rank != root:
        pack_x()

    t.wait_ge(T.sem.qs, 4)
    t.wait_ge(T.sem.in_w, 32)
    for b in range(4):
        t.matmul_mx(T.acc[:, 512 * b:512 * b + 128], T.sc[:, 128 * b:128 * b + 128], T.ss[:, 128 * b:128 * b + 128],
                    T.pc[:], T.ps[:], True, True).then_inc(T.sem.dd, 1)
    t.wait_ge(T.sem.qb, 4)
    if rank == root:
        t.wait_ge(T.sem.qa, 1)
    else:
        t.wait_ge(T.sem.arr_a, 2 * count(out))
    for b in (0, 2, 1, 3):
        t.matmul_mx(T.acc[:, 512 * (4 + b):512 * (4 + b) + 128], T.bc[:, 128 * b:128 * b + 128], T.bs[:, 128 * b:128 * b + 128],
                    T.ac[:], T.as_[:], True, True).then_inc(T.sem["ba%d" % b], 1)

    def prod(b):
        return T.acc[:, 512 * (4 + b):512 * (4 + b) + 128]

    def scaled(b):
        return T.m[:, 128 * b:128 * b + 128]

    for b in (2, 3):
        s.wait_ge(T.sem["ba%d" % b], 1)
        s.activation(scaled(b), prod(b), ActivationFunctionType.Copy, scale=C).then_inc(T.sem["ml%d" % b], 1)
    v.wait_ge(T.sem.dd, 4)
    for b in (0, 1):
        v.wait_ge(T.sem["ba%d" % b], 1)
        v.tensor_scalar(scaled(b), prod(b), C, None, AluOpType.mult).then_inc(T.sem["ml%d" % b], 1)
    for b in (0, 1, 2, 3):
        v.wait_ge(T.sem["ml%d" % b], 1)
        v.tensor_tensor(T.vt[:, b:512:4], T.acc[:, 512 * b:512 * b + 128], scaled(b), AluOpType.add).then_inc(T.sem.ad, 1)
    v.wait_ge(T.sem.ad, 4)
    v.quantize_mx(T.vc[:, 128 * rank:128 * rank + 128], T.vs[:, 128 * rank:128 * rank + 128], T.vt[:]).then_inc(T.sem.qv, 1)
    if rank == root:
        pack_x()

    g.wait_ge(T.sem.one, 1)
    g.affine_select(T.eye[:], T.eye[:], [[-1, 516]], AluOpType.is_equal, 0.0, 3, 4).then_inc(T.sem.sel, 1)
    if rank == root:
        g.wait_ge(T.sem.qa, 1)
        for kind in "cs":
            send(move(kind, aland(kind), [(k, rland(kind, 0)) for k in relays_of(rank, kind)], T.sem.rel_a, full))
        for kind in "cs":
            send(move(kind, aland(kind), [(cores[d], aland(kind)) for d in near[rank]], T.sem.arr_a, out))
    g.wait_ge(T.sem.qv, 1)
    for kind in "cs":
        send(move(kind, vland(kind, rank), [(k, rland(kind, 1)) for k in relays_of(rank, kind)], T.sem.rel_v, rest),
             move(kind, vland(kind, rank), [(cores[d], vland(kind, rank)) for d in near[rank]], T.sem["v%d" % rank], out))

    t.wait_ge(T.sem.qx, 1)
    stores = [0, 0]
    for i, j in enumerate(order):
        if j == rank:
            t.wait_ge(T.sem.qv, 1)
        else:
            t.wait_ge(T.sem["v%d" % j], 2 * count(out))
        res = T.acc[:, 512 * i:512 * i + NX]
        t.matmul_mx(res, T.vc[:, 128 * j:128 * j + 128], T.vs[:, 128 * j:128 * j + 128], T.xc[:], T.xs[:], True, True).then_inc(T.sem["my%d" % i], 1)
        dst = T.yo[:, NX * j:NX * j + NX]
        e = v if i % 2 else s
        q = g.sync if i % 2 else s
        e.wait_ge(T.sem["my%d" % i], 1)
        if i % 2:
            v.tensor_copy(dst, res).then_inc(T.sem["cy%d" % i], 1)
        else:
            s.activation(dst, res, ActivationFunctionType.Copy).then_inc(T.sem["cy%d" % i], 1)
        q.wait_ge(T.sem["cy%d" % i], 1)
        q.dma_start(T.y[:, NX * j:NX * j + NX], dst).then_inc(T.sem.st_s if i % 2 else T.sem.st_a, 16)
        stores[i % 2] += 16
    s.wait_ge(T.sem.st_a, stores[0])
    g.sync.wait_ge(T.sem.st_s, stores[1])
    g.wait_ge(T.sem.loc, loc[0])
